import numpy as np
import ml_dtypes


def mxq(x, axis, fmt="e4m3"):
    dtype, down = {"e4m3": (ml_dtypes.float8_e4m3fn, 7), "e5m2": (ml_dtypes.float8_e5m2, 14)}[fmt]
    v = np.moveaxis(np.asarray(x, np.float32).astype(ml_dtypes.bfloat16).astype(np.float64), axis, -1)
    blocks = v.reshape(v.shape[:-1] + (-1, 32))
    amax = np.abs(blocks).max(-1, keepdims=True)
    byte = np.maximum(np.where(amax > 0, np.frexp(amax)[1] - 1 + 127, 0) - down, 1)
    scale = np.exp2(byte - 127.0)
    codes = (blocks / scale).astype(np.float32).astype(dtype).astype(np.float64)
    return np.moveaxis((codes * scale).reshape(v.shape), -1, axis)


WIDE = False


def mx_kscale(k):
    if not WIDE:
        return np.ones(k)
    levels = np.array([10, -10, 5, -5, 0])
    if k % 512:
        return np.exp2(np.random.permutation(np.resize(levels, k // 32))).repeat(32)
    a = np.empty((k // 512, 16))
    for p in range(k // 512):
        a[p, :8] = np.random.permutation(np.resize(levels, 8))
        for g in range(8):
            far = levels[np.abs(levels - a[p, g]) >= 10]
            a[p, g + 8] = far[np.random.randint(len(far))]
    return np.exp2(a.ravel()).repeat(32)


BF16 = ml_dtypes.bfloat16


def bf(x):
    return np.asarray(x, np.float32).astype(BF16)


def f64(x):
    return np.asarray(x).astype(np.float64)


E2M1 = np.array([0.0, 0.5, 1.0, 1.5, 2.0, 3.0, 4.0, 6.0, -0.0, -0.5, -1.0, -1.5, -2.0, -3.0, -4.0, -6.0])


def pack_weight(w, fmt):
    k, n = w.shape
    w = f64(bf(w)).reshape(k // 32, 32, n)
    amax = np.abs(w).max(1)
    if fmt == "e4m3":
        byte = np.frexp(amax)[1] - 1 + 127 - 7
    else:
        mant, ex = np.frexp(amax / 6.0)
        byte = np.where(mant > 0.5, ex, ex - 1) + 127
    byte = np.clip(np.where(amax > 0, byte, 1), 1, 254)
    scaled = (w * np.exp2(127.0 - byte)[:, None, :]).reshape(k, n).astype(np.float32)
    by_word = np.ascontiguousarray(scaled.reshape(k // 512, 128, 4, n).transpose(0, 1, 3, 2))
    if fmt == "e4m3":
        words = by_word.astype(ml_dtypes.float8_e4m3fn).view(np.uint8)
    else:
        c = by_word.astype(ml_dtypes.float4_e2m1fn).view(np.uint8) & 0xF
        words = c[..., 0::2] | (c[..., 1::2] << 4)
    return np.ascontiguousarray(words), np.ascontiguousarray(byte.astype(np.uint8).reshape(k // 512, 16, n))


def unpack_weight(words, scales, fmt):
    g, p, n, _ = words.shape
    if fmt == "e4m3":
        vals = np.ascontiguousarray(words).view(ml_dtypes.float8_e4m3fn).astype(np.float64)
    else:
        nib = np.empty((g, p, n, 4), np.uint8)
        nib[..., 0::2] = words & 0xF
        nib[..., 1::2] = words >> 4
        vals = E2M1[nib]
    vals = vals * np.repeat(np.exp2(scales.astype(np.float64) - 127.0), 8, axis=1)[..., None]
    return vals.transpose(0, 1, 3, 2).reshape(g * 512, n)
def pack4(w):
    words, scales = pack_weight(w, "e2m1")
    return words.reshape(words.shape[0], 128, -1), scales


def unpack4(words, scales):
    return unpack_weight(words.reshape(words.shape[0], 128, -1, 2), scales, "e2m1")


def planes(Y):
    n, m = Y.shape
    b = f64(bf(Y)).reshape(n // 32, 32, m)
    amax = np.abs(b).max(1)
    byte = np.clip(np.where(amax > 0, np.frexp(amax)[1] - 1 + 127 - 7, 1), 1, 254)
    codes = (b * np.exp2(127.0 - byte)[:, None, :]).reshape(n, m).astype(np.float32).astype(ml_dtypes.float8_e4m3fn).view(np.uint8)
    words = codes.reshape(n // 512, 128, 4, m).transpose(0, 1, 3, 2)
    return np.ascontiguousarray(words), np.ascontiguousarray(byte.astype(np.uint8).reshape(n // 512, 16, m))


G, R, N, F = 4, 512, 1024, 512

def setup_inputs():
    s, t = mx_kscale(N), mx_kscale(F)
    size = np.exp(0.6 * np.random.randn(G, 1, N)) * np.exp(-2.5 * np.arange(N) / N)
    z = size * np.random.randn(G, R, N)
    dual = np.tanh(z)
    older = np.tanh(z + 0.5 * size * np.random.randn(G, R, N))
    dual_bar = dual + (dual - older)
    image = 0.8 * np.random.randn(G, R, F)
    D = np.random.randn(G, N, F) / np.sqrt(F)
    tau = 0.4 * size
    B = D / s[:, None] * t
    C = D.swapaxes(1, 2) * tau / t[:, None]
    B_words, B_scales = pack4(B.reshape(G * N, F))
    C_words, C_scales = pack4(C.reshape(G * F, N))
    return {"dual": bf(dual), "dual_bar": bf(dual_bar * s), "image": bf(image * t),
            "B_words": B_words, "B_scales": B_scales, "C_words": C_words, "C_scales": C_scales}

def reference(dual, dual_bar, image, B_words, B_scales, C_words, C_scales):
    B = unpack4(B_words, B_scales).reshape(G, N, F)
    C = unpack4(C_words, C_scales).reshape(G, F, N)
    r = (mxq(f64(dual_bar), 2, "e4m3") @ B) - f64(image)
    h = mxq(r, 2, "e4m3") @ C
    y = (f64(dual) - h) / (1.0 + np.abs(h))
    Y = y.reshape(G * R, N).T
    words, scales = planes(Y)
    return y, words, scales

@@ -1,0 +1,315 @@
+from contextlib import ExitStack
+
+import concourse.mybir as mybir
+from concourse.masks import make_identity
+
+G, R, N, F = 4, 512, 1024, 512
+FLOPS = 2 * 2 * G * R * N * F
+
+F32 = mybir.dt.float32
+BF16 = mybir.dt.bfloat16
+I32 = mybir.dt.int32
+U32 = mybir.dt.uint32
+U8 = mybir.dt.uint8
+FP8X4 = mybir.dt.float8_e4m3fn_x4
+FP4X4 = mybir.dt.float4_e2m1fn_x4
+ALU = mybir.AluOpType
+ACT = mybir.ActivationFunctionType
+
+P = 128
+BANK = 512
+TILES = G * R // P
+PER_GROUP = R // P
+SPLIT = 512
+LOAD_LEAD = 3
+
+
+def tile_chambolle_type_dual_step_k7_kernel(
+    tc, dual, dual_bar, image, B_words, B_scales, C_words, C_scales, out_0, out_1, out_2
+):
+    nc = tc.nc
+    dual_rows = dual.rearrange("g r n -> (g r) n")
+    bar_rows = dual_bar.rearrange("g r n -> (g r) n")
+    image_rows = image.rearrange("g r f -> (g r) f")
+    y_rows = out_0.rearrange("g r n -> (g r) n")
+
+    with ExitStack() as ctx:
+        keep = ctx.enter_context(tc.tile_pool(name="keep", bufs=1))
+        work = ctx.enter_context(tc.tile_pool(name="work", bufs=2))
+        psum = ctx.enter_context(tc.psum_pool(name="psum", bufs=1))
+        ctx.enter_context(tc.manual_schedule())
+
+        t = {}
+
+        def rows(i):
+            return slice(P * i, P * (i + 1))
+
+        ident = keep.tile([P, P], F32, name="ident")
+        warm = keep.tile([P, 8], F32, name="warm")
+        warm_out = keep.tile([P, 8], F32, name="warm_out")
+        y_scales = keep.tile([P, 2, G * R], U8, name="y_scales", align_bytes=64)
+        b_scale = [
+            keep.tile([P, 2, F], U8, name="b_scale_first", align_bytes=64),
+            keep.tile([P, 2 * (G - 1), F], U8, name="b_scale_rest", align_bytes=64),
+        ]
+        c_scale = [
+            keep.tile([P, 1, N], U8, name="c_scale_first", align_bytes=64),
+            keep.tile([P, G - 1, N], U8, name="c_scale_rest", align_bytes=64),
+        ]
+
+        def load_scales(plane, src, first, count):
+            for quad in range(4):
+                nc.sync.dma_start(
+                    out=plane[32 * quad : 32 * quad + 4, :, :].bitcast(I32),
+                    in_=src[first : first + count, 4 * quad : 4 * quad + 4, :].rearrange("g r n -> r g n").bitcast(I32),
+                )
+
+        def load_b(j):
+            w = keep.tile([P, 2, 2 * F], U8, name="b_words%d" % j, align_bytes=64)
+            nc.sync.dma_start(out=w[:].bitcast(I32), in_=B_words[2 * j : 2 * j + 2].rearrange("g p n -> p g n").bitcast(I32))
+            t["bw", j] = w
+
+        def load_c(j):
+            w = keep.tile([P, 2 * N], U8, name="c_words%d" % j, align_bytes=64)
+            nc.sync.dma_start(out=w[:].bitcast(I32), in_=C_words[j].bitcast(I32))
+            t["cw", j] = w
+
+        def load_bar(i):
+            x = work.tile([P, N], BF16, name="bar", bufs=8)
+            nc.sync.dma_start(out=x[:], in_=bar_rows[rows(i), :])
+            t["bar", i] = x
+
+        def load_image(i):
+            x = work.tile([P, F], BF16, name="img", bufs=8)
+            nc.sync.dma_start(out=x[:], in_=image_rows[rows(i), :])
+            t["img", i] = x
+
+        def load_dual(i):
+            x = work.tile([P, N], BF16, name="dual_in", bufs=8)
+            nc.sync.dma_start(out=x[:], in_=dual_rows[rows(i), :])
+            t["dual", i] = x
+
+        def turn_bar(i):
+            bank = psum.tile([P, 4, P], F32, name="bar_t")
+            words = t["bar", i][:].bitcast(F32)
+            for g in range(2):
+                for u in range(2):
+                    nc.tensor.transpose(bank[:, 2 * g + u, :], words[:, 256 * g + u : 256 * (g + 1) : 2], ident[:])
+            t["bar_t", i] = bank
+            t["bar_k", i] = work.tile([P, 2, 4 * P], BF16, name="bar_k", align_bytes=64)
+
+        def copy_bar(i, g):
+            nc.scalar.copy(
+                out=t["bar_k", i][:, g, :].bitcast(F32).rearrange("p (r u) -> p r u", u=2),
+                in_=t["bar_t", i][:, 2 * g : 2 * g + 2, :].rearrange("p u r -> p r u"),
+            )
+
+        def quantize_bar(i):
+            codes = work.tile([P, 2 * P], U32, name="bar_codes", bufs=3, align_bytes=64)
+            scales = work.tile([P, 2 * P], U8, name="bar_scales", bufs=3, align_bytes=64)
+            nc.vector.quantize_mx(
+                out=codes[:].bitcast(FP8X4), scales=scales[:], in_=t["bar_k", i][:].rearrange("p g c -> p (g c)")
+            )
+            t["bar_q", i] = (codes, scales)
+
+        def first_product(i):
+            j = i // PER_GROUP
+            codes, scales = t["bar_q", i]
+            bank = psum.tile([P, F], F32, name="r_acc")
+            for g in range(2):
+                plane = b_scale[0][:, g, :] if j == 0 else b_scale[1][:, 2 * (j - 1) + g, :]
+                nc.tensor.matmul_mx(
+                    out=bank[:],
+                    lhsT=codes[:, P * g : P * (g + 1)].bitcast(FP8X4),
+                    lhsT_scale=scales[:, P * g : P * (g + 1)],
+                    rhs=t["bw", j][:, g, :].bitcast(FP4X4),
+                    rhs_scale=plane,
+                    start=(g == 0),
+                    stop=(g == 1),
+                )
+            t["r_acc", i] = bank
+
+        def residual(i):
+            r = work.tile([P, F], BF16, name="r", bufs=3, align_bytes=64)
+            nc.vector.tensor_tensor(
+                out=r[:].rearrange("p (u q e) -> p u q e", u=2, e=2),
+                in0=t["r_acc", i][:].rearrange("p (q u e) -> p u q e", u=2, e=2),
+                in1=t["img", i][:].rearrange("p (q u e) -> p u q e", u=2, e=2),
+                op=ALU.subtract,
+            )
+            t["r", i] = r
+
+        def turn_r(i):
+            bank = psum.tile([P, 2, P], F32, name="r_t")
+            words = t["r", i][:].bitcast(F32)
+            for u in range(2):
+                nc.tensor.transpose(bank[:, u, :], words[:, P * u : P * (u + 1)], ident[:])
+            t["r_t", i] = bank
+
+        def copy_r(i):
+            x = work.tile([P, 4 * P], BF16, name="r_k", align_bytes=64)
+            nc.vector.tensor_copy(
+                out=x[:].bitcast(F32).rearrange("p (r u) -> p r u", u=2),
+                in_=t["r_t", i][:].rearrange("p u r -> p r u"),
+            )
+            t["r_k", i] = x
+
+        def quantize_r(i):
+            codes = work.tile([P, P], U32, name="r_codes", align_bytes=64)
+            scales = work.tile([P, P], U8, name="r_scales", align_bytes=64)
+            nc.vector.quantize_mx(out=codes[:].bitcast(FP8X4), scales=scales[:], in_=t["r_k", i][:])
+            t["r_q", i] = (codes, scales)
+
+        def second_product(i):
+            j = i // PER_GROUP
+            codes, scales = t["r_q", i]
+            plane = c_scale[0][:, 0, :] if j == 0 else c_scale[1][:, j - 1, :]
+            for b in range(2):
+                bank = psum.tile([P, BANK], F32, name="h%d" % b, bufs=2)
+                nc.tensor.matmul_mx(
+                    out=bank[:],
+                    lhsT=codes[:].bitcast(FP8X4),
+                    lhsT_scale=scales[:],
+                    rhs=t["cw", j][:, 2 * BANK * b : 2 * BANK * (b + 1)].bitcast(FP4X4),
+                    rhs_scale=plane[:, BANK * b : BANK * (b + 1)],
+                    start=True,
+                    stop=True,
+                )
+                t["h", i, b] = bank
+
+        def magnitude(i):
+            mag = work.tile([P, N], F32, name="mag")
+            for b in range(2):
+                nc.scalar.activation(out=mag[:, BANK * b : BANK * (b + 1)], in_=t["h", i, b][:], func=ACT.Abs)
+            t["mag", i] = mag
+
+        def numerator(i):
+            d = work.tile([P, N], F32, name="num", bufs=3)
+            for b in range(2):
+                cols = slice(BANK * b, BANK * (b + 1))
+                nc.vector.tensor_tensor(out=d[:, cols], in0=t["dual", i][:, cols], in1=t["h", i, b][:], op=ALU.subtract)
+            t["num", i] = d
+
+        def inverse_root(i):
+            q = work.tile([P, N], F32, name="root")
+            nc.scalar.activation(out=q[:], in_=t["mag", i][:], func=ACT.Abs_reciprocal_sqrt, bias=1.0)
+            t["root", i] = q
+
+        def inverse(i):
+            s = work.tile([P, N], F32, name="inv", bufs=3)
+            nc.scalar.activation(out=s[:], in_=t["root", i][:], func=ACT.Square)
+            t["inv", i] = s
+
+        def new_dual(i):
+            y = work.tile([P, N], F32, name="y", bufs=4)
+            yb = work.tile([P, N], BF16, name="y_bf16", bufs=3)
+            d, s = t["num", i], t["inv", i]
+            nc.vector.tensor_tensor(out=y[:, :SPLIT], in0=d[:, :SPLIT], in1=s[:, :SPLIT], op=ALU.mult)
+            nc.gpsimd.tensor_scalar(out=yb[:, :SPLIT], in0=y[:, :SPLIT], scalar1=1.0, scalar2=1.0, op0=ALU.mult, op1=ALU.mult)
+            nc.gpsimd.tensor_tensor(out=y[:, SPLIT:], in0=d[:, SPLIT:], in1=s[:, SPLIT:], op=ALU.mult)
+            nc.gpsimd.tensor_scalar(out=yb[:, SPLIT:], in0=y[:, SPLIT:], scalar1=1.0, scalar2=1.0, op0=ALU.mult, op1=ALU.mult)
+            nc.sync.dma_start(out=y_rows[rows(i), :], in_=y[:])
+            t["yb", i] = yb
+
+        def turn_y(i):
+            bank = psum.tile([P, 4, P], F32, name="y_t")
+            words = t["yb", i][:].bitcast(F32)
+            for g in range(2):
+                for u in range(2):
+                    nc.tensor.transpose(bank[:, 2 * g + u, :], words[:, 256 * g + u : 256 * (g + 1) : 2], ident[:])
+            t["y_t", i] = bank
+
+        def copy_y(i):
+            x = work.tile([P, 2, 4 * P], BF16, name="y_k", align_bytes=64)
+            nc.vector.tensor_copy(
+                out=x[:].bitcast(F32).rearrange("p g (r u) -> p g r u", u=2),
+                in_=t["y_t", i][:].rearrange("p (g u) r -> p g r u", u=2),
+            )
+            t["y_k", i] = x
+
+        def store_planes(j, first, last):
+            lo, hi = P * first, P * (last + 1)
+            base = R * j
+            nc.sync.dma_start(
+                out=out_1[:, :, lo:hi, :].rearrange("g p m t -> p g (m t)").bitcast(I32),
+                in_=t["y_codes", j][:, :, lo - base : hi - base].bitcast(I32),
+            )
+
+        def store_scales(first, last):
+            lo, hi = P * first, P * (last + 1)
+            for quad in range(4):
+                nc.sync.dma_start(
+                    out=out_2[:, 4 * quad : 4 * quad + 4, lo:hi].rearrange("g r m -> r g m").bitcast(I32),
+                    in_=y_scales[32 * quad : 32 * quad + 4, :, lo:hi].bitcast(I32),
+                )
+
+        def quantize_y(i):
+            j, k = divmod(i, PER_GROUP)
+            if k == 0:
+                t["y_codes", j] = work.tile([P, 2, R], U32, name="y_codes", align_bytes=64)
+            for g in range(2):
+                nc.vector.quantize_mx(
+                    out=t["y_codes", j][:, g, P * k : P * (k + 1)].bitcast(FP8X4),
+                    scales=y_scales[:, g, rows(i)],
+                    in_=t["y_k", i][:, g, :],
+                )
+            if i == TILES - 2:
+                store_planes(j, PER_GROUP * j, i)
+                store_scales(0, i)
+            elif i == TILES - 1:
+                store_planes(j, i, i)
+                store_scales(i, i)
+            elif k == PER_GROUP - 1:
+                store_planes(j, PER_GROUP * j, i)
+
+        def on(fn, i, *rest):
+            if 0 <= i < TILES:
+                fn(i, *rest)
+
+        nc.vector.memset(b_scale[0][:].bitcast(I32), 0)
+        nc.vector.memset(c_scale[0][:].bitcast(I32), 0)
+        nc.vector.memset(warm[:], 1.0)
+        nc.vector.memset(b_scale[1][:].bitcast(I32), 0)
+        nc.vector.memset(c_scale[1][:].bitcast(I32), 0)
+        nc.scalar.activation(out=warm_out[:], in_=warm[:], func=ACT.Abs_reciprocal_sqrt)
+        make_identity(nc, ident[:])
+        load_bar(0)
+        load_scales(b_scale[0], B_scales, 0, 2)
+        load_b(0)
+        load_bar(1)
+        load_image(0)
+        load_scales(c_scale[0], C_scales, 0, 1)
+        load_c(0)
+        load_bar(2)
+        load_image(1)
+        load_dual(0)
+
+        for n in range(-3, TILES + 2):
+            on(load_bar, n + 3 + LOAD_LEAD)
+            on(load_image, n + 2 + LOAD_LEAD)
+            on(load_dual, n + 1 + LOAD_LEAD)
+            if n == -2:
+                load_scales(b_scale[1], B_scales, 2, 2 * (G - 1))
+            if n == -1:
+                load_scales(c_scale[1], C_scales, 1, G - 1)
+            if n % PER_GROUP == PER_GROUP - 1 and n // PER_GROUP + 2 < G:
+                load_b(n // PER_GROUP + 2)
+                load_c(n // PER_GROUP + 2)
+            on(new_dual, n - 1)
+            on(turn_r, n + 1)
+            on(turn_bar, n + 3)
+            on(turn_y, n - 2)
+            on(magnitude, n)
+            on(numerator, n)
+            on(copy_bar, n + 3, 0)
+            on(inverse_root, n)
+            on(copy_bar, n + 3, 1)
+            on(inverse, n)
+            on(copy_r, n + 1)
+            on(copy_y, n - 2)
+            on(first_product, n + 2)
+            on(residual, n + 2)
+            on(quantize_r, n + 1)
+            on(second_product, n + 1)
+            on(quantize_bar, n + 3)
+            on(quantize_y, n - 2)

@@ -20,8 +20,9 @@ P = 128
 BANK = 512
 TILES = G * R // P
 PER_GROUP = R // P
-SPLIT = 512
-LOAD_LEAD = 3
+D_ON_S = [6, 9, 13, 15]
+L_ON_S = [14]
+SPLITS = [576] * 12 + [1024] * 4
 
 
 def tile_chambolle_type_dual_step_k7_kernel(
@@ -47,7 +48,10 @@ def tile_chambolle_type_dual_step_k7_kernel(
         ident = keep.tile([P, P], F32, name="ident")
         warm = keep.tile([P, 8], F32, name="warm")
         warm_out = keep.tile([P, 8], F32, name="warm_out")
-        y_scales = keep.tile([P, 2, G * R], U8, name="y_scales", align_bytes=64)
+        y_scales = [
+            keep.tile([P, 2, (G - 1) * R], U8, name="y_scales_first", align_bytes=64),
+            keep.tile([P, 2, R], U8, name="y_scales_last", align_bytes=64),
+        ]
         b_scale = [
             keep.tile([P, 2, F], U8, name="b_scale_first", align_bytes=64),
             keep.tile([P, 2 * (G - 1), F], U8, name="b_scale_rest", align_bytes=64),
@@ -90,7 +94,7 @@ def tile_chambolle_type_dual_step_k7_kernel(
             t["dual", i] = x
 
         def turn_bar(i):
-            bank = psum.tile([P, 4, P], F32, name="bar_t")
+            bank = psum.tile([P, 4, P], F32, name="y_t" if i == 1 else "bar_t")
             words = t["bar", i][:].bitcast(F32)
             for g in range(2):
                 for u in range(2):
@@ -148,7 +152,7 @@ def tile_chambolle_type_dual_step_k7_kernel(
 
         def copy_r(i):
             x = work.tile([P, 4 * P], BF16, name="r_k", align_bytes=64)
-            nc.vector.tensor_copy(
+            (nc.scalar.copy if i in D_ON_S else nc.vector.tensor_copy)(
                 out=x[:].bitcast(F32).rearrange("p (r u) -> p r u", u=2),
                 in_=t["r_t", i][:].rearrange("p u r -> p r u"),
             )
@@ -160,107 +164,115 @@ def tile_chambolle_type_dual_step_k7_kernel(
             nc.vector.quantize_mx(out=codes[:].bitcast(FP8X4), scales=scales[:], in_=t["r_k", i][:])
             t["r_q", i] = (codes, scales)
 
-        def second_product(i):
+        def second_product(i, b):
             j = i // PER_GROUP
             codes, scales = t["r_q", i]
             plane = c_scale[0][:, 0, :] if j == 0 else c_scale[1][:, j - 1, :]
-            for b in range(2):
-                bank = psum.tile([P, BANK], F32, name="h%d" % b, bufs=2)
-                nc.tensor.matmul_mx(
-                    out=bank[:],
-                    lhsT=codes[:].bitcast(FP8X4),
-                    lhsT_scale=scales[:],
-                    rhs=t["cw", j][:, 2 * BANK * b : 2 * BANK * (b + 1)].bitcast(FP4X4),
-                    rhs_scale=plane[:, BANK * b : BANK * (b + 1)],
-                    start=True,
-                    stop=True,
-                )
-                t["h", i, b] = bank
+            bank = psum.tile([P, BANK], F32, name="h", bufs=4)
+            nc.tensor.matmul_mx(
+                out=bank[:],
+                lhsT=codes[:].bitcast(FP8X4),
+                lhsT_scale=scales[:],
+                rhs=t["cw", j][:, 2 * BANK * b : 2 * BANK * (b + 1)].bitcast(FP4X4),
+                rhs_scale=plane[:, BANK * b : BANK * (b + 1)],
+                start=True,
+                stop=True,
+            )
+            t["h", i, b] = bank
 
-        def magnitude(i):
-            mag = work.tile([P, N], F32, name="mag")
-            for b in range(2):
-                nc.scalar.activation(out=mag[:, BANK * b : BANK * (b + 1)], in_=t["h", i, b][:], func=ACT.Abs)
-            t["mag", i] = mag
+        def half(b):
+            return slice(BANK * b, BANK * (b + 1))
 
-        def numerator(i):
-            d = work.tile([P, N], F32, name="num", bufs=3)
-            for b in range(2):
-                cols = slice(BANK * b, BANK * (b + 1))
-                nc.vector.tensor_tensor(out=d[:, cols], in0=t["dual", i][:, cols], in1=t["h", i, b][:], op=ALU.subtract)
-            t["num", i] = d
+        def magnitude(i, b):
+            if b == 0:
+                t["mag", i] = work.tile([P, N], F32, name="mag")
+            nc.scalar.activation(out=t["mag", i][:, half(b)], in_=t["h", i, b][:], func=ACT.Abs)
 
-        def inverse_root(i):
-            q = work.tile([P, N], F32, name="root")
-            nc.scalar.activation(out=q[:], in_=t["mag", i][:], func=ACT.Abs_reciprocal_sqrt, bias=1.0)
-            t["root", i] = q
+        def numerator(i, b):
+            if b == 0:
+                t["num", i] = work.tile([P, N], F32, name="num", bufs=3)
+            nc.vector.tensor_tensor(out=t["num", i][:, half(b)], in0=t["dual", i][:, half(b)], in1=t["h", i, b][:], op=ALU.subtract)
 
-        def inverse(i):
-            s = work.tile([P, N], F32, name="inv", bufs=3)
-            nc.scalar.activation(out=s[:], in_=t["root", i][:], func=ACT.Square)
-            t["inv", i] = s
+        def inverse_root(i, lo, hi):
+            if lo == 0:
+                t["root", i] = work.tile([P, N], F32, name="root")
+            nc.scalar.activation(out=t["root", i][:, lo:hi], in_=t["mag", i][:, lo:hi], func=ACT.Abs_reciprocal_sqrt, bias=1.0)
 
-        def new_dual(i):
-            y = work.tile([P, N], F32, name="y", bufs=4)
-            yb = work.tile([P, N], BF16, name="y_bf16", bufs=3)
-            d, s = t["num", i], t["inv", i]
-            nc.vector.tensor_tensor(out=y[:, :SPLIT], in0=d[:, :SPLIT], in1=s[:, :SPLIT], op=ALU.mult)
-            nc.gpsimd.tensor_scalar(out=yb[:, :SPLIT], in0=y[:, :SPLIT], scalar1=1.0, scalar2=1.0, op0=ALU.mult, op1=ALU.mult)
-            nc.gpsimd.tensor_tensor(out=y[:, SPLIT:], in0=d[:, SPLIT:], in1=s[:, SPLIT:], op=ALU.mult)
-            nc.gpsimd.tensor_scalar(out=yb[:, SPLIT:], in0=y[:, SPLIT:], scalar1=1.0, scalar2=1.0, op0=ALU.mult, op1=ALU.mult)
-            nc.sync.dma_start(out=y_rows[rows(i), :], in_=y[:])
-            t["yb", i] = yb
+        def inverse(i, lo, hi):
+            if lo == 0:
+                t["inv", i] = work.tile([P, N], F32, name="inv", bufs=3)
+            nc.scalar.activation(out=t["inv", i][:, lo:hi], in_=t["root", i][:, lo:hi], func=ACT.Square)
 
-        def turn_y(i):
-            bank = psum.tile([P, 4, P], F32, name="y_t")
+        def new_dual(i, lo, hi, engine):
+            if lo == 0:
+                t["y", i] = work.tile([P, N], F32, name="y", bufs=4)
+                t["yb", i] = work.tile([P, N], BF16, name="y_bf16", bufs=3)
+            engine.tensor_tensor(out=t["y", i][:, lo:hi], in0=t["num", i][:, lo:hi], in1=t["inv", i][:, lo:hi], op=ALU.mult)
+
+        def store_y(i, lo, hi):
+            nc.sync.dma_start(out=y_rows[rows(i), lo:hi], in_=t["y", i][:, lo:hi])
+
+        def round_y(i, lo, hi, engine):
+            engine.tensor_scalar(out=t["yb", i][:, lo:hi], in0=t["y", i][:, lo:hi], scalar1=1.0, scalar2=1.0, op0=ALU.mult, op1=ALU.mult)
+
+        def turn_y(i, g):
+            if g == 0:
+                t["y_t", i] = psum.tile([P, 4, P], F32, name="y_t")
             words = t["yb", i][:].bitcast(F32)
-            for g in range(2):
-                for u in range(2):
-                    nc.tensor.transpose(bank[:, 2 * g + u, :], words[:, 256 * g + u : 256 * (g + 1) : 2], ident[:])
-            t["y_t", i] = bank
+            for u in range(2):
+                nc.tensor.transpose(t["y_t", i][:, 2 * g + u, :], words[:, 256 * g + u : 256 * (g + 1) : 2], ident[:])
 
         def copy_y(i):
             x = work.tile([P, 2, 4 * P], BF16, name="y_k", align_bytes=64)
-            nc.vector.tensor_copy(
+            (nc.scalar.copy if i in L_ON_S else nc.vector.tensor_copy)(
                 out=x[:].bitcast(F32).rearrange("p g (r u) -> p g r u", u=2),
                 in_=t["y_t", i][:].rearrange("p (g u) r -> p g r u", u=2),
             )
             t["y_k", i] = x
 
-        def store_planes(j, first, last):
-            lo, hi = P * first, P * (last + 1)
-            base = R * j
-            nc.sync.dma_start(
-                out=out_1[:, :, lo:hi, :].rearrange("g p m t -> p g (m t)").bitcast(I32),
-                in_=t["y_codes", j][:, :, lo - base : hi - base].bitcast(I32),
+        def turn_last(i, g):
+            bank = psum.tile([P, 2, P], F32, name=("r_t", "bar_t")[g])
+            words = t["yb", i][:].bitcast(F32)
+            for u in range(2):
+                nc.tensor.transpose(bank[:, u, :], words[:, 256 * g + u : 256 * (g + 1) : 2], ident[:])
+            if g == 0:
+                t["y_k", i] = work.tile([P, 2, 4 * P], BF16, name="y_k", align_bytes=64)
+            nc.scalar.copy(
+                out=t["y_k", i][:, g, :].bitcast(F32).rearrange("p (r u) -> p r u", u=2),
+                in_=bank[:, 0:2, :].rearrange("p u r -> p r u"),
             )
 
-        def store_scales(first, last):
+        def store_words(first, last, groups):
+            j = first // PER_GROUP
             lo, hi = P * first, P * (last + 1)
+            nc.sync.dma_start(
+                out=out_1[groups, :, lo:hi, :].rearrange("g p m t -> p g (m t)").bitcast(I32),
+                in_=t["y_codes", j][:, groups, lo - R * j : hi - R * j].bitcast(I32),
+            )
+
+        def store_scales(plane, first, last, queues):
             for quad in range(4):
-                nc.sync.dma_start(
-                    out=out_2[:, 4 * quad : 4 * quad + 4, lo:hi].rearrange("g r m -> r g m").bitcast(I32),
-                    in_=y_scales[32 * quad : 32 * quad + 4, :, lo:hi].bitcast(I32),
+                queues[quad].dma_start(
+                    out=out_2[:, 4 * quad : 4 * quad + 4, P * first : P * (last + 1)].rearrange("g r m -> r g m").bitcast(I32),
+                    in_=plane[32 * quad : 32 * quad + 4, :, :].bitcast(I32),
                 )
 
-        def quantize_y(i):
+        def quantize_y(i, g):
             j, k = divmod(i, PER_GROUP)
-            if k == 0:
+            if k == 0 and g == 0:
                 t["y_codes", j] = work.tile([P, 2, R], U32, name="y_codes", align_bytes=64)
-            for g in range(2):
-                nc.vector.quantize_mx(
-                    out=t["y_codes", j][:, g, P * k : P * (k + 1)].bitcast(FP8X4),
-                    scales=y_scales[:, g, rows(i)],
-                    in_=t["y_k", i][:, g, :],
-                )
+            plane = y_scales[1][:, g, rows(k)] if j == G - 1 else y_scales[0][:, g, rows(i)]
+            nc.vector.quantize_mx(
+                out=t["y_codes", j][:, g, rows(k)].bitcast(FP8X4), scales=plane, in_=t["y_k", i][:, g, :]
+            )
+
+        def store_group(i):
+            if i % PER_GROUP == PER_GROUP - 1:
+                store_words(i + 1 - PER_GROUP, i, slice(0, 2))
+            if i == TILES - PER_GROUP - 1:
+                store_scales(y_scales[0], 0, i, [nc.sync] * 4)
             if i == TILES - 2:
-                store_planes(j, PER_GROUP * j, i)
-                store_scales(0, i)
-            elif i == TILES - 1:
-                store_planes(j, i, i)
-                store_scales(i, i)
-            elif k == PER_GROUP - 1:
-                store_planes(j, PER_GROUP * j, i)
+                store_words(TILES - PER_GROUP, i, slice(0, 2))
 
         def on(fn, i, *rest):
             if 0 <= i < TILES:
@@ -282,34 +294,117 @@ def tile_chambolle_type_dual_step_k7_kernel(
         load_c(0)
         load_bar(2)
         load_image(1)
+        load_bar(3)
         load_dual(0)
+        load_image(2)
+        load_bar(4)
+        load_image(3)
+        load_dual(1)
+        load_bar(5)
+        load_scales(b_scale[1], B_scales, 2, 2 * (G - 1))
+        load_b(1)
+        load_image(4)
+        load_dual(2)
+        load_bar(6)
+        load_scales(c_scale[1], C_scales, 1, G - 1)
+        load_c(1)
 
-        for n in range(-3, TILES + 2):
-            on(load_bar, n + 3 + LOAD_LEAD)
-            on(load_image, n + 2 + LOAD_LEAD)
-            on(load_dual, n + 1 + LOAD_LEAD)
-            if n == -2:
-                load_scales(b_scale[1], B_scales, 2, 2 * (G - 1))
-            if n == -1:
-                load_scales(c_scale[1], C_scales, 1, G - 1)
-            if n % PER_GROUP == PER_GROUP - 1 and n // PER_GROUP + 2 < G:
+        def copy_bar_both(i):
+            copy_bar(i, 0)
+            copy_bar(i, 1)
+
+        turn_bar(0)
+        turn_bar(1)
+        copy_bar_both(0)
+        quantize_bar(0)
+        first_product(0)
+        copy_bar_both(1)
+        turn_bar(2)
+        residual(0)
+        quantize_bar(1)
+        turn_r(0)
+        first_product(1)
+        copy_bar_both(2)
+        copy_r(0)
+        quantize_r(0)
+        turn_bar(3)
+        second_product(0, 0)
+        second_product(0, 1)
+        residual(1)
+        quantize_bar(2)
+        turn_r(1)
+        first_product(2)
+        copy_bar_both(3)
+        turn_bar(4)
+        copy_r(1)
+        residual(2)
+        quantize_r(1)
+
+        last = TILES - 1
+        for n in range(TILES):
+            split = SPLITS[n - 1]
+            on(load_bar, n + 7)
+            on(load_image, n + 5)
+            on(load_dual, n + 3)
+            if n % PER_GROUP == 0 and n // PER_GROUP + 2 < G:
                 load_b(n // PER_GROUP + 2)
                 load_c(n // PER_GROUP + 2)
-            on(new_dual, n - 1)
-            on(turn_r, n + 1)
-            on(turn_bar, n + 3)
-            on(turn_y, n - 2)
-            on(magnitude, n)
-            on(numerator, n)
-            on(copy_bar, n + 3, 0)
-            on(inverse_root, n)
-            on(copy_bar, n + 3, 1)
-            on(inverse, n)
-            on(copy_r, n + 1)
-            on(copy_y, n - 2)
-            on(first_product, n + 2)
-            on(residual, n + 2)
-            on(quantize_r, n + 1)
-            on(second_product, n + 1)
+            on(new_dual, n - 1, 0, split, nc.vector)
             on(quantize_bar, n + 3)
-            on(quantize_y, n - 2)
+            on(round_y, n - 1, 0, split, nc.gpsimd)
+            if split < N:
+                on(new_dual, n - 1, split, N, nc.gpsimd)
+                on(round_y, n - 1, split, N, nc.gpsimd)
+            on(store_y, n - 1, 0, N)
+            on(turn_r, n + 2)
+            on(turn_y, n - 2, 0)
+            on(turn_y, n - 2, 1)
+            magnitude(n, 0)
+            magnitude(n, 1)
+            on(copy_r, n + 2)
+            numerator(n, 0)
+            if n - 2 not in L_ON_S:
+                on(copy_y, n - 2)
+            numerator(n, 1)
+            if n + 4 < TILES:
+                copy_bar(n + 4, 0)
+                inverse_root(n, 0, N)
+                copy_bar(n + 4, 1)
+                if n - 2 in L_ON_S:
+                    copy_y(n - 2)
+                inverse(n, 0, N)
+            else:
+                inverse_root(n, 0, BANK)
+                inverse_root(n, BANK, N)
+                if n - 2 in L_ON_S:
+                    copy_y(n - 2)
+                inverse(n, 0, BANK)
+                inverse(n, BANK, N)
+            on(second_product, n + 1, 0)
+            on(first_product, n + 3)
+            on(second_product, n + 1, 1)
+            on(turn_bar, n + 5)
+            on(residual, n + 3)
+            on(quantize_r, n + 2)
+            on(quantize_y, n - 2, 0)
+            on(quantize_y, n - 2, 1)
+            on(store_group, n - 2)
+
+        turn_y(last - 1, 0)
+        turn_y(last - 1, 1)
+        copy_y(last - 1)
+        t["y", last] = work.tile([P, N], F32, name="y", bufs=4)
+        t["yb", last] = work.tile([P, N], BF16, name="y_bf16", bufs=3)
+        for b in range(2):
+            nc.vector.tensor_tensor(out=t["yb", last][:, half(b)], in0=t["num", last][:, half(b)], in1=t["inv", last][:, half(b)], op=ALU.mult)
+            turn_last(last, b)
+        for b in range(2):
+            nc.vector.tensor_tensor(out=t["y", last][:, half(b)], in0=t["num", last][:, half(b)], in1=t["inv", last][:, half(b)], op=ALU.mult)
+            store_y(last, BANK * b, BANK * (b + 1))
+        for b in range(2):
+            quantize_y(last - 1, b)
+        store_group(last - 1)
+        for b in range(2):
+            quantize_y(last, b)
+        store_words(last, last, slice(0, 2))
+        store_scales(y_scales[1], TILES - PER_GROUP, last, [nc.scalar, nc.scalar, nc.sync, nc.sync])

@@ -17,12 +17,17 @@ ALU = mybir.AluOpType
 ACT = mybir.ActivationFunctionType
 
 P = 128
-BANK = 512
+HALF = 512
+PAIRS = HALF // 2
 TILES = G * R // P
 PER_GROUP = R // P
-D_ON_S = [6, 9, 13, 15]
-L_ON_S = [14]
-SPLITS = [576] * 12 + [1024] * 4
+LAST = TILES - 1
+
+BANKS = {"bar_t": 1, "r_acc": 1, "r_t": 1, "y_t": 1, "h": 4}
+
+VECTOR_COLUMNS = 608
+VECTOR_ALONE_FROM = 12
+SCALAR_COPIES_R_FROM = 9
 
 
 def tile_chambolle_type_dual_step_k7_kernel(
@@ -33,6 +38,7 @@ def tile_chambolle_type_dual_step_k7_kernel(
     bar_rows = dual_bar.rearrange("g r n -> (g r) n")
     image_rows = image.rearrange("g r f -> (g r) f")
     y_rows = out_0.rearrange("g r n -> (g r) n")
+    on_vector, on_scalar = nc.vector.tensor_copy, nc.scalar.copy
 
     with ExitStack() as ctx:
         keep = ctx.enter_context(tc.tile_pool(name="keep", bufs=1))
@@ -40,214 +46,196 @@ def tile_chambolle_type_dual_step_k7_kernel(
         psum = ctx.enter_context(tc.psum_pool(name="psum", bufs=1))
         ctx.enter_context(tc.manual_schedule())
 
-        t = {}
+        made = {}
+
+        ident = keep.tile([P, P], F32, name="ident")
+        y_all = keep.tile([P, TILES * N], F32, name="y_all")
+        y_bf16 = keep.tile([P, TILES * N], BF16, name="y_bf16")
+        y_scales_early = keep.tile([P, 2, (G - 1) * R], U8, name="y_scales_early", align_bytes=64)
+        y_scales_last = keep.tile([P, 2, R], U8, name="y_scales_last", align_bytes=64)
 
         def rows(i):
             return slice(P * i, P * (i + 1))
 
-        ident = keep.tile([P, P], F32, name="ident")
-        warm = keep.tile([P, 8], F32, name="warm")
-        warm_out = keep.tile([P, 8], F32, name="warm_out")
-        y_scales = [
-            keep.tile([P, 2, (G - 1) * R], U8, name="y_scales_first", align_bytes=64),
-            keep.tile([P, 2, R], U8, name="y_scales_last", align_bytes=64),
-        ]
-        b_scale = [
-            keep.tile([P, 2, F], U8, name="b_scale_first", align_bytes=64),
-            keep.tile([P, 2 * (G - 1), F], U8, name="b_scale_rest", align_bytes=64),
-        ]
-        c_scale = [
-            keep.tile([P, 1, N], U8, name="c_scale_first", align_bytes=64),
-            keep.tile([P, G - 1, N], U8, name="c_scale_rest", align_bytes=64),
-        ]
+        def half(b):
+            return slice(HALF * b, HALF * (b + 1))
 
-        def load_scales(plane, src, first, count):
-            for quad in range(4):
-                nc.sync.dma_start(
-                    out=plane[32 * quad : 32 * quad + 4, :, :].bitcast(I32),
-                    in_=src[first : first + count, 4 * quad : 4 * quad + 4, :].rearrange("g r n -> r g n").bitcast(I32),
-                )
+        def bank(tag, shape):
+            return psum.tile(shape, F32, name=tag, bufs=BANKS[tag])
+
+        def clear_scales(j):
+            made["scales", j] = keep.tile([P, 2 * F + N], U8, name="scales%d" % j, align_bytes=64)
+            nc.vector.memset(made["scales", j][:].bitcast(I32), 0)
 
         def load_b(j):
-            w = keep.tile([P, 2, 2 * F], U8, name="b_words%d" % j, align_bytes=64)
-            nc.sync.dma_start(out=w[:].bitcast(I32), in_=B_words[2 * j : 2 * j + 2].rearrange("g p n -> p g n").bitcast(I32))
-            t["bw", j] = w
+            for quad in range(4):
+                nc.sync.dma_start(
+                    out=made["scales", j][32 * quad : 32 * quad + 4, : 2 * F].rearrange("r (g n) -> r g n", g=2).bitcast(I32),
+                    in_=B_scales[2 * j : 2 * j + 2, 4 * quad : 4 * quad + 4, :].rearrange("g r n -> r g n").bitcast(I32),
+                )
+            words = keep.tile([P, 2, 2 * F], U8, name="b_words%d" % j, align_bytes=64)
+            nc.sync.dma_start(out=words[:].bitcast(I32), in_=B_words[2 * j : 2 * j + 2].rearrange("g p n -> p g n").bitcast(I32))
+            made["b_words", j] = words
 
         def load_c(j):
-            w = keep.tile([P, 2 * N], U8, name="c_words%d" % j, align_bytes=64)
-            nc.sync.dma_start(out=w[:].bitcast(I32), in_=C_words[j].bitcast(I32))
-            t["cw", j] = w
+            for quad in range(4):
+                nc.sync.dma_start(
+                    out=made["scales", j][32 * quad : 32 * quad + 4, 2 * F :].bitcast(I32),
+                    in_=C_scales[j, 4 * quad : 4 * quad + 4, :].bitcast(I32),
+                )
+            words = keep.tile([P, 2 * N], U8, name="c_words%d" % j, align_bytes=64)
+            nc.sync.dma_start(out=words[:].bitcast(I32), in_=C_words[j].bitcast(I32))
+            made["c_words", j] = words
+
+        def load_rows(what, source, i, bufs):
+            made[what, i] = work.tile([P, source.shape[1]], BF16, name=what, bufs=bufs)
+            nc.sync.dma_start(out=made[what, i][:], in_=source[rows(i), :])
 
         def load_bar(i):
-            x = work.tile([P, N], BF16, name="bar", bufs=8)
-            nc.sync.dma_start(out=x[:], in_=bar_rows[rows(i), :])
-            t["bar", i] = x
+            load_rows("bar", bar_rows, i, 8)
 
         def load_image(i):
-            x = work.tile([P, F], BF16, name="img", bufs=8)
-            nc.sync.dma_start(out=x[:], in_=image_rows[rows(i), :])
-            t["img", i] = x
+            load_rows("image", image_rows, i, 7)
 
         def load_dual(i):
-            x = work.tile([P, N], BF16, name="dual_in", bufs=8)
-            nc.sync.dma_start(out=x[:], in_=dual_rows[rows(i), :])
-            t["dual", i] = x
+            load_rows("dual", dual_rows, i, 4)
 
-        def turn_bar(i):
-            bank = psum.tile([P, 4, P], F32, name="y_t" if i == 1 else "bar_t")
-            words = t["bar", i][:].bitcast(F32)
-            for g in range(2):
+        def turn(pairs, passes, tag):
+            turned = bank(tag, [P, 2 * len(passes), P])
+            for s, g in enumerate(passes):
                 for u in range(2):
-                    nc.tensor.transpose(bank[:, 2 * g + u, :], words[:, 256 * g + u : 256 * (g + 1) : 2], ident[:])
-            t["bar_t", i] = bank
-            t["bar_k", i] = work.tile([P, 2, 4 * P], BF16, name="bar_k", align_bytes=64)
+                    nc.tensor.transpose(turned[:, 2 * s + u, :], pairs[:, PAIRS * g + u : PAIRS * (g + 1) : 2], ident[:])
+            return turned
 
-        def copy_bar(i, g):
-            nc.scalar.copy(
-                out=t["bar_k", i][:, g, :].bitcast(F32).rearrange("p (r u) -> p r u", u=2),
-                in_=t["bar_t", i][:, 2 * g : 2 * g + 2, :].rearrange("p u r -> p r u"),
+        def interleave(copy, name, turned, bufs):
+            ordered = work.tile([P, turned.shape[1] // 2, HALF], BF16, name=name, bufs=bufs, align_bytes=64)
+            copy(
+                out=ordered[:].bitcast(F32).rearrange("p g (r u) -> p g r u", u=2),
+                in_=turned[:].rearrange("p (g u) r -> p g r u", u=2),
             )
+            return ordered
+
+        def quantize(name, ordered, bufs):
+            width = ordered.shape[1] * P
+            codes = work.tile([P, width], U32, name=name + "_codes", bufs=bufs, align_bytes=64)
+            scales = work.tile([P, width], U8, name=name + "_scales", bufs=bufs, align_bytes=64)
+            nc.vector.quantize_mx(out=codes[:].bitcast(FP8X4), scales=scales[:], in_=ordered[:].rearrange("p g c -> p (g c)"))
+            return codes, scales
+
+        def turn_bar(i, tag="bar_t"):
+            made["bar_t", i] = turn(made["bar", i][:].bitcast(F32), [0, 1], tag)
+
+        def copy_bar(i, copy=on_scalar):
+            made["bar_k", i] = interleave(copy, "bar_k", made["bar_t", i], 4)
 
         def quantize_bar(i):
-            codes = work.tile([P, 2 * P], U32, name="bar_codes", bufs=3, align_bytes=64)
-            scales = work.tile([P, 2 * P], U8, name="bar_scales", bufs=3, align_bytes=64)
-            nc.vector.quantize_mx(
-                out=codes[:].bitcast(FP8X4), scales=scales[:], in_=t["bar_k", i][:].rearrange("p g c -> p (g c)")
-            )
-            t["bar_q", i] = (codes, scales)
+            made["bar_q", i] = quantize("bar", made["bar_k", i], 3)
 
-        def first_product(i):
+        def first_product(i, tag="r_acc"):
             j = i // PER_GROUP
-            codes, scales = t["bar_q", i]
-            bank = psum.tile([P, F], F32, name="r_acc")
+            codes, scales = made["bar_q", i]
+            acc = bank(tag, [P, F])
             for g in range(2):
-                plane = b_scale[0][:, g, :] if j == 0 else b_scale[1][:, 2 * (j - 1) + g, :]
                 nc.tensor.matmul_mx(
-                    out=bank[:],
-                    lhsT=codes[:, P * g : P * (g + 1)].bitcast(FP8X4),
-                    lhsT_scale=scales[:, P * g : P * (g + 1)],
-                    rhs=t["bw", j][:, g, :].bitcast(FP4X4),
-                    rhs_scale=plane,
+                    out=acc[:],
+                    lhsT=codes[:, rows(g)].bitcast(FP8X4),
+                    lhsT_scale=scales[:, rows(g)],
+                    rhs=made["b_words", j][:, g, :].bitcast(FP4X4),
+                    rhs_scale=made["scales", j][:, F * g : F * (g + 1)],
                     start=(g == 0),
                     stop=(g == 1),
                 )
-            t["r_acc", i] = bank
+            made["r_acc", i] = acc
 
         def residual(i):
-            r = work.tile([P, F], BF16, name="r", bufs=3, align_bytes=64)
+            r = work.tile([P, F], BF16, name="r", bufs=4)
             nc.vector.tensor_tensor(
-                out=r[:].rearrange("p (u q e) -> p u q e", u=2, e=2),
-                in0=t["r_acc", i][:].rearrange("p (q u e) -> p u q e", u=2, e=2),
-                in1=t["img", i][:].rearrange("p (q u e) -> p u q e", u=2, e=2),
+                out=r[:].rearrange("m (u p e) -> m u p e", u=2, e=2),
+                in0=made["r_acc", i][:].rearrange("m (p u e) -> m u p e", u=2, e=2),
+                in1=made["image", i][:].rearrange("m (p u e) -> m u p e", u=2, e=2),
                 op=ALU.subtract,
             )
-            t["r", i] = r
+            made["r", i] = r
 
-        def turn_r(i):
-            bank = psum.tile([P, 2, P], F32, name="r_t")
-            words = t["r", i][:].bitcast(F32)
+        def turn_r(i, tag="r_t"):
+            turned = bank(tag, [P, 2, P])
+            pairs = made["r", i][:].bitcast(F32)
             for u in range(2):
-                nc.tensor.transpose(bank[:, u, :], words[:, P * u : P * (u + 1)], ident[:])
-            t["r_t", i] = bank
+                nc.tensor.transpose(turned[:, u, :], pairs[:, rows(u)], ident[:])
+            made["r_t", i] = turned
 
-        def copy_r(i):
-            x = work.tile([P, 4 * P], BF16, name="r_k", align_bytes=64)
-            (nc.scalar.copy if i in D_ON_S else nc.vector.tensor_copy)(
-                out=x[:].bitcast(F32).rearrange("p (r u) -> p r u", u=2),
-                in_=t["r_t", i][:].rearrange("p u r -> p r u"),
-            )
-            t["r_k", i] = x
+        def copy_r(i, copy):
+            made["r_k", i] = interleave(copy, "r_k", made["r_t", i], 2)
 
         def quantize_r(i):
-            codes = work.tile([P, P], U32, name="r_codes", align_bytes=64)
-            scales = work.tile([P, P], U8, name="r_scales", align_bytes=64)
-            nc.vector.quantize_mx(out=codes[:].bitcast(FP8X4), scales=scales[:], in_=t["r_k", i][:])
-            t["r_q", i] = (codes, scales)
+            made["r_q", i] = quantize("r", made["r_k", i], 4)
 
         def second_product(i, b):
             j = i // PER_GROUP
-            codes, scales = t["r_q", i]
-            plane = c_scale[0][:, 0, :] if j == 0 else c_scale[1][:, j - 1, :]
-            bank = psum.tile([P, BANK], F32, name="h", bufs=4)
+            codes, scales = made["r_q", i]
+            acc = bank("h", [P, HALF])
             nc.tensor.matmul_mx(
-                out=bank[:],
+                out=acc[:],
                 lhsT=codes[:].bitcast(FP8X4),
                 lhsT_scale=scales[:],
-                rhs=t["cw", j][:, 2 * BANK * b : 2 * BANK * (b + 1)].bitcast(FP4X4),
-                rhs_scale=plane[:, BANK * b : BANK * (b + 1)],
+                rhs=made["c_words", j][:, 2 * HALF * b : 2 * HALF * (b + 1)].bitcast(FP4X4),
+                rhs_scale=made["scales", j][:, 2 * F + HALF * b : 2 * F + HALF * (b + 1)],
                 start=True,
                 stop=True,
             )
-            t["h", i, b] = bank
-
-        def half(b):
-            return slice(BANK * b, BANK * (b + 1))
+            made["h", i, b] = acc
 
         def magnitude(i, b):
             if b == 0:
-                t["mag", i] = work.tile([P, N], F32, name="mag")
-            nc.scalar.activation(out=t["mag", i][:, half(b)], in_=t["h", i, b][:], func=ACT.Abs)
+                made["mag", i] = work.tile([P, N], F32, name="mag")
+            nc.scalar.activation(out=made["mag", i][:, half(b)], in_=made["h", i, b][:], func=ACT.Abs)
 
         def numerator(i, b):
             if b == 0:
-                t["num", i] = work.tile([P, N], F32, name="num", bufs=3)
-            nc.vector.tensor_tensor(out=t["num", i][:, half(b)], in0=t["dual", i][:, half(b)], in1=t["h", i, b][:], op=ALU.subtract)
+                made["num", i] = work.tile([P, N], F32, name="num", bufs=3)
+            nc.vector.tensor_tensor(
+                out=made["num", i][:, half(b)], in0=made["dual", i][:, half(b)], in1=made["h", i, b][:], op=ALU.subtract
+            )
 
         def inverse_root(i, lo, hi):
             if lo == 0:
-                t["root", i] = work.tile([P, N], F32, name="root")
-            nc.scalar.activation(out=t["root", i][:, lo:hi], in_=t["mag", i][:, lo:hi], func=ACT.Abs_reciprocal_sqrt, bias=1.0)
+                made["root", i] = work.tile([P, N], F32, name="root")
+            nc.scalar.activation(
+                out=made["root", i][:, lo:hi], in_=made["mag", i][:, lo:hi], func=ACT.Abs_reciprocal_sqrt, bias=1.0
+            )
 
         def inverse(i, lo, hi):
             if lo == 0:
-                t["inv", i] = work.tile([P, N], F32, name="inv", bufs=3)
-            nc.scalar.activation(out=t["inv", i][:, lo:hi], in_=t["root", i][:, lo:hi], func=ACT.Square)
+                made["inv", i] = work.tile([P, N], F32, name="inv", bufs=3)
+            nc.scalar.activation(out=made["inv", i][:, lo:hi], in_=made["root", i][:, lo:hi], func=ACT.Square)
 
-        def new_dual(i, lo, hi, engine):
-            if lo == 0:
-                t["y", i] = work.tile([P, N], F32, name="y", bufs=4)
-                t["yb", i] = work.tile([P, N], BF16, name="y_bf16", bufs=3)
-            engine.tensor_tensor(out=t["y", i][:, lo:hi], in0=t["num", i][:, lo:hi], in1=t["inv", i][:, lo:hi], op=ALU.mult)
+        def new_dual(engine, into, i, lo, hi):
+            engine.tensor_tensor(
+                out=into[:, N * i + lo : N * i + hi], in0=made["num", i][:, lo:hi], in1=made["inv", i][:, lo:hi], op=ALU.mult
+            )
 
         def store_y(i, lo, hi):
-            nc.sync.dma_start(out=y_rows[rows(i), lo:hi], in_=t["y", i][:, lo:hi])
+            nc.sync.dma_start(out=y_rows[rows(i), lo:hi], in_=y_all[:, N * i + lo : N * i + hi])
 
-        def round_y(i, lo, hi, engine):
-            engine.tensor_scalar(out=t["yb", i][:, lo:hi], in0=t["y", i][:, lo:hi], scalar1=1.0, scalar2=1.0, op0=ALU.mult, op1=ALU.mult)
-
-        def turn_y(i, g):
-            if g == 0:
-                t["y_t", i] = psum.tile([P, 4, P], F32, name="y_t")
-            words = t["yb", i][:].bitcast(F32)
-            for u in range(2):
-                nc.tensor.transpose(t["y_t", i][:, 2 * g + u, :], words[:, 256 * g + u : 256 * (g + 1) : 2], ident[:])
-
-        def copy_y(i):
-            x = work.tile([P, 2, 4 * P], BF16, name="y_k", align_bytes=64)
-            (nc.scalar.copy if i in L_ON_S else nc.vector.tensor_copy)(
-                out=x[:].bitcast(F32).rearrange("p g (r u) -> p g r u", u=2),
-                in_=t["y_t", i][:].rearrange("p (g u) r -> p g r u", u=2),
-            )
-            t["y_k", i] = x
-
-        def turn_last(i, g):
-            bank = psum.tile([P, 2, P], F32, name=("r_t", "bar_t")[g])
-            words = t["yb", i][:].bitcast(F32)
-            for u in range(2):
-                nc.tensor.transpose(bank[:, u, :], words[:, 256 * g + u : 256 * (g + 1) : 2], ident[:])
-            if g == 0:
-                t["y_k", i] = work.tile([P, 2, 4 * P], BF16, name="y_k", align_bytes=64)
-            nc.scalar.copy(
-                out=t["y_k", i][:, g, :].bitcast(F32).rearrange("p (r u) -> p r u", u=2),
-                in_=bank[:, 0:2, :].rearrange("p u r -> p r u"),
+        def round_y(lo, hi):
+            nc.gpsimd.tensor_scalar(
+                out=y_bf16[:, lo:hi], in0=y_all[:, lo:hi], scalar1=1.0, scalar2=1.0, op0=ALU.mult, op1=ALU.mult
             )
 
-        def store_words(first, last, groups):
+        def turn_y(halves, tag):
+            made["y_t", halves[0]] = turn(y_bf16[:].bitcast(F32), halves, tag)
+
+        def copy_y(halves, copy):
+            ordered = interleave(copy, "y_k", made["y_t", halves[0]], 4)
+            for s, h in enumerate(halves):
+                made["y_k", h] = ordered[:, s, :]
+
+        def store_words(first, last):
             j = first // PER_GROUP
             lo, hi = P * first, P * (last + 1)
             nc.sync.dma_start(
-                out=out_1[groups, :, lo:hi, :].rearrange("g p m t -> p g (m t)").bitcast(I32),
-                in_=t["y_codes", j][:, groups, lo - R * j : hi - R * j].bitcast(I32),
+                out=out_1[:, :, lo:hi, :].rearrange("g p m t -> p g (m t)").bitcast(I32),
+                in_=made["y_codes", j][:, :, lo - R * j : hi - R * j].bitcast(I32),
             )
 
         def store_scales(plane, first, last, queues):
@@ -257,154 +245,155 @@ def tile_chambolle_type_dual_step_k7_kernel(
                     in_=plane[32 * quad : 32 * quad + 4, :, :].bitcast(I32),
                 )
 
-        def quantize_y(i, g):
+        def quantize_y(h):
+            i, g = divmod(h, 2)
             j, k = divmod(i, PER_GROUP)
             if k == 0 and g == 0:
-                t["y_codes", j] = work.tile([P, 2, R], U32, name="y_codes", align_bytes=64)
-            plane = y_scales[1][:, g, rows(k)] if j == G - 1 else y_scales[0][:, g, rows(i)]
-            nc.vector.quantize_mx(
-                out=t["y_codes", j][:, g, rows(k)].bitcast(FP8X4), scales=plane, in_=t["y_k", i][:, g, :]
-            )
+                made["y_codes", j] = work.tile([P, 2, R], U32, name="y_codes", align_bytes=64)
+            plane = y_scales_last[:, g, rows(k)] if j == G - 1 else y_scales_early[:, g, rows(i)]
+            nc.vector.quantize_mx(out=made["y_codes", j][:, g, rows(k)].bitcast(FP8X4), scales=plane, in_=made["y_k", h])
+            if g == 1 and k == PER_GROUP - 1 and j < G - 1:
+                store_words(PER_GROUP * j, i)
+            if g == 1 and i == LAST - PER_GROUP:
+                store_scales(y_scales_early, 0, i, [nc.sync] * 4)
+            if g == 1 and i == LAST - 2:
+                store_words(PER_GROUP * j, i)
 
-        def store_group(i):
-            if i % PER_GROUP == PER_GROUP - 1:
-                store_words(i + 1 - PER_GROUP, i, slice(0, 2))
-            if i == TILES - PER_GROUP - 1:
-                store_scales(y_scales[0], 0, i, [nc.sync] * 4)
-            if i == TILES - 2:
-                store_words(TILES - PER_GROUP, i, slice(0, 2))
-
-        def on(fn, i, *rest):
+        def on(step, i, *rest):
             if 0 <= i < TILES:
-                fn(i, *rest)
+                step(i, *rest)
 
-        nc.vector.memset(b_scale[0][:].bitcast(I32), 0)
-        nc.vector.memset(c_scale[0][:].bitcast(I32), 0)
-        nc.vector.memset(warm[:], 1.0)
-        nc.vector.memset(b_scale[1][:].bitcast(I32), 0)
-        nc.vector.memset(c_scale[1][:].bitcast(I32), 0)
-        nc.scalar.activation(out=warm_out[:], in_=warm[:], func=ACT.Abs_reciprocal_sqrt)
+        clear_scales(0)
+        warm_in = keep.tile([P, 8], F32, name="warm_in")
+        warm_out = keep.tile([P, 8], F32, name="warm_out")
+        nc.vector.memset(warm_in[:], 1.0)
+        nc.scalar.activation(out=warm_out[:], in_=warm_in[:], func=ACT.Abs_reciprocal_sqrt)
         make_identity(nc, ident[:])
+        for j in range(1, G):
+            clear_scales(j)
+
         load_bar(0)
-        load_scales(b_scale[0], B_scales, 0, 2)
         load_b(0)
         load_bar(1)
         load_image(0)
-        load_scales(c_scale[0], C_scales, 0, 1)
-        load_c(0)
         load_bar(2)
         load_image(1)
+        load_c(0)
         load_bar(3)
         load_dual(0)
         load_image(2)
         load_bar(4)
-        load_image(3)
         load_dual(1)
-        load_bar(5)
-        load_scales(b_scale[1], B_scales, 2, 2 * (G - 1))
+        load_image(3)
         load_b(1)
+        load_bar(5)
         load_image(4)
-        load_dual(2)
         load_bar(6)
-        load_scales(c_scale[1], C_scales, 1, G - 1)
-        load_c(1)
 
-        def copy_bar_both(i):
-            copy_bar(i, 0)
-            copy_bar(i, 1)
-
-        turn_bar(0)
-        turn_bar(1)
-        copy_bar_both(0)
+        turn_bar(0, "r_acc")
+        copy_bar(0, on_vector)
         quantize_bar(0)
-        first_product(0)
-        copy_bar_both(1)
-        turn_bar(2)
-        residual(0)
+        turn_bar(1, "h")
+        first_product(0, "bar_t")
+        copy_bar(1, on_vector)
         quantize_bar(1)
-        turn_r(0)
-        first_product(1)
-        copy_bar_both(2)
-        copy_r(0)
+        first_product(1, "r_t")
+        residual(0)
+        turn_r(0, "bar_t")
+        residual(1)
+        copy_r(0, on_scalar)
+        turn_bar(2, "r_acc")
         quantize_r(0)
-        turn_bar(3)
+        copy_bar(2, on_vector)
+        turn_bar(3, "h")
+        turn_r(1, "y_t")
+        copy_bar(3, on_vector)
         second_product(0, 0)
         second_product(0, 1)
-        residual(1)
         quantize_bar(2)
-        turn_r(1)
-        first_product(2)
-        copy_bar_both(3)
-        turn_bar(4)
-        copy_r(1)
-        residual(2)
+        turn_bar(4, "r_t")
+        magnitude(0, 0)
+        copy_r(1, on_vector)
         quantize_r(1)
+        first_product(2, "y_t")
+        residual(2)
 
-        last = TILES - 1
+        rounded = 0
+        turned = 0
         for n in range(TILES):
-            split = SPLITS[n - 1]
+            ready = list(range(turned, rounded // HALF))
+            turned += len(ready)
+            two, third = ready[:2], ready[2:]
+            split = VECTOR_COLUMNS if n - 1 < VECTOR_ALONE_FROM else N
+            r_copy_on_scalar = n + 2 >= SCALAR_COPIES_R_FROM
+
             on(load_bar, n + 7)
             on(load_image, n + 5)
-            on(load_dual, n + 3)
-            if n % PER_GROUP == 0 and n // PER_GROUP + 2 < G:
-                load_b(n // PER_GROUP + 2)
-                load_c(n // PER_GROUP + 2)
-            on(new_dual, n - 1, 0, split, nc.vector)
-            on(quantize_bar, n + 3)
-            on(round_y, n - 1, 0, split, nc.gpsimd)
-            if split < N:
-                on(new_dual, n - 1, split, N, nc.gpsimd)
-                on(round_y, n - 1, split, N, nc.gpsimd)
-            on(store_y, n - 1, 0, N)
-            on(turn_r, n + 2)
-            on(turn_y, n - 2, 0)
-            on(turn_y, n - 2, 1)
-            magnitude(n, 0)
+            on(load_dual, n + 2)
+            if (n + 5) % PER_GROUP == 0 and n + 5 < TILES:
+                load_b((n + 5) // PER_GROUP)
+            if (n + 3) % PER_GROUP == 0 and n + 3 < TILES:
+                load_c((n + 3) // PER_GROUP)
+
+            if two:
+                turn_y(two, "y_t")
+            if third:
+                turn_y(third, "bar_t")
             magnitude(n, 1)
-            on(copy_r, n + 2)
-            numerator(n, 0)
-            if n - 2 not in L_ON_S:
-                on(copy_y, n - 2)
-            numerator(n, 1)
-            if n + 4 < TILES:
-                copy_bar(n + 4, 0)
-                inverse_root(n, 0, N)
-                copy_bar(n + 4, 1)
-                if n - 2 in L_ON_S:
-                    copy_y(n - 2)
-                inverse(n, 0, N)
-            else:
-                inverse_root(n, 0, BANK)
-                inverse_root(n, BANK, N)
-                if n - 2 in L_ON_S:
-                    copy_y(n - 2)
-                inverse(n, 0, BANK)
-                inverse(n, BANK, N)
+            if n == LAST:
+                copy_y(two, on_scalar)
+            if n > 0:
+                new_dual(nc.vector, y_all, n - 1, 0, split)
+            on(quantize_bar, n + 3)
             on(second_product, n + 1, 0)
-            on(first_product, n + 3)
+            if n + 4 < TILES:
+                copy_bar(n + 4)
+                inverse_root(n, 0, N)
+            else:
+                inverse_root(n, 0, HALF)
+                inverse_root(n, HALF, N)
+            on(turn_r, n + 2)
             on(second_product, n + 1, 1)
+            if third:
+                copy_y(third, on_vector)
+            if r_copy_on_scalar:
+                on(copy_r, n + 2, on_scalar)
+            on(first_product, n + 3)
+            numerator(n, 0)
+            if not r_copy_on_scalar:
+                copy_r(n + 2, on_vector)
+            if two and n < LAST:
+                copy_y(two, on_vector)
+            on(magnitude, n + 1, 0)
             on(turn_bar, n + 5)
+            numerator(n, 1)
             on(residual, n + 3)
             on(quantize_r, n + 2)
-            on(quantize_y, n - 2, 0)
-            on(quantize_y, n - 2, 1)
-            on(store_group, n - 2)
+            if n > 0:
+                round_y(rounded, N * (n - 1) + split)
+                rounded = N * (n - 1) + split
+                if split < N:
+                    new_dual(nc.gpsimd, y_all, n - 1, split, N)
+                store_y(n - 1, 0, N)
+            if n < LAST:
+                inverse(n, 0, N)
+            else:
+                inverse(n, 0, HALF)
+                inverse(n, HALF, N)
+            for h in ready:
+                quantize_y(h)
 
-        turn_y(last - 1, 0)
-        turn_y(last - 1, 1)
-        copy_y(last - 1)
-        t["y", last] = work.tile([P, N], F32, name="y", bufs=4)
-        t["yb", last] = work.tile([P, N], BF16, name="y_bf16", bufs=3)
+        before_last = list(range(turned, 2 * LAST))
+        turn_y(before_last, "y_t")
+        copy_y(before_last, on_scalar)
+        for b, tag in enumerate(["r_t", "bar_t"]):
+            new_dual(nc.vector, y_bf16, LAST, HALF * b, HALF * (b + 1))
+            turn_y([2 * LAST + b], tag)
+            copy_y([2 * LAST + b], on_scalar)
         for b in range(2):
-            nc.vector.tensor_tensor(out=t["yb", last][:, half(b)], in0=t["num", last][:, half(b)], in1=t["inv", last][:, half(b)], op=ALU.mult)
-            turn_last(last, b)
-        for b in range(2):
-            nc.vector.tensor_tensor(out=t["y", last][:, half(b)], in0=t["num", last][:, half(b)], in1=t["inv", last][:, half(b)], op=ALU.mult)
-            store_y(last, BANK * b, BANK * (b + 1))
-        for b in range(2):
-            quantize_y(last - 1, b)
-        store_group(last - 1)
-        for b in range(2):
-            quantize_y(last, b)
-        store_words(last, last, slice(0, 2))
-        store_scales(y_scales[1], TILES - PER_GROUP, last, [nc.scalar, nc.scalar, nc.sync, nc.sync])
+            new_dual(nc.vector, y_all, LAST, HALF * b, HALF * (b + 1))
+            store_y(LAST, HALF * b, HALF * (b + 1))
+        for h in range(turned, 2 * TILES):
+            quantize_y(h)
+        store_words(LAST - 1, LAST)
+        store_scales(y_scales_last, TILES - PER_GROUP, LAST, [nc.scalar, nc.scalar, nc.sync, nc.sync])

from contextlib import ExitStack

import concourse.mybir as mybir
from concourse.masks import make_identity

G, R, N, F = 4, 512, 1024, 512
FLOPS = 2 * 2 * G * R * N * F

F32 = mybir.dt.float32
BF16 = mybir.dt.bfloat16
I32 = mybir.dt.int32
U32 = mybir.dt.uint32
U8 = mybir.dt.uint8
FP8X4 = mybir.dt.float8_e4m3fn_x4
FP4X4 = mybir.dt.float4_e2m1fn_x4
ALU = mybir.AluOpType
ACT = mybir.ActivationFunctionType

P = 128
HALF = 512
PAIRS = HALF // 2
TILES = G * R // P
PER_GROUP = R // P
LAST = TILES - 1

BANKS = {"bar_t": 1, "r_acc": 1, "r_t": 1, "y_t": 1, "h": 4}

VECTOR_COLUMNS = 608
VECTOR_ALONE_FROM = 12
SCALAR_COPIES_R_FROM = 9


def tile_chambolle_type_dual_step_k7_kernel(
    tc, dual, dual_bar, image, B_words, B_scales, C_words, C_scales, out_0, out_1, out_2
):
    nc = tc.nc
    dual_rows = dual.rearrange("g r n -> (g r) n")
    bar_rows = dual_bar.rearrange("g r n -> (g r) n")
    image_rows = image.rearrange("g r f -> (g r) f")
    y_rows = out_0.rearrange("g r n -> (g r) n")
    on_vector, on_scalar = nc.vector.tensor_copy, nc.scalar.copy

    with ExitStack() as ctx:
        keep = ctx.enter_context(tc.tile_pool(name="keep", bufs=1))
        work = ctx.enter_context(tc.tile_pool(name="work", bufs=2))
        psum = ctx.enter_context(tc.psum_pool(name="psum", bufs=1))
        ctx.enter_context(tc.manual_schedule())

        made = {}

        ident = keep.tile([P, P], F32, name="ident")
        y_all = keep.tile([P, TILES * N], F32, name="y_all")
        y_bf16 = keep.tile([P, TILES * N], BF16, name="y_bf16")
        y_scales_early = keep.tile([P, 2, (G - 1) * R], U8, name="y_scales_early", align_bytes=64)
        y_scales_last = keep.tile([P, 2, R], U8, name="y_scales_last", align_bytes=64)

        def rows(i):
            return slice(P * i, P * (i + 1))

        def half(b):
            return slice(HALF * b, HALF * (b + 1))

        def bank(tag, shape):
            return psum.tile(shape, F32, name=tag, bufs=BANKS[tag])

        def clear_scales(j):
            made["scales", j] = keep.tile([P, 2 * F + N], U8, name="scales%d" % j, align_bytes=64)
            nc.vector.memset(made["scales", j][:].bitcast(I32), 0)

        def load_b(j):
            for quad in range(4):
                nc.sync.dma_start(
                    out=made["scales", j][32 * quad : 32 * quad + 4, : 2 * F].rearrange("r (g n) -> r g n", g=2).bitcast(I32),
                    in_=B_scales[2 * j : 2 * j + 2, 4 * quad : 4 * quad + 4, :].rearrange("g r n -> r g n").bitcast(I32),
                )
            words = keep.tile([P, 2, 2 * F], U8, name="b_words%d" % j, align_bytes=64)
            nc.sync.dma_start(out=words[:].bitcast(I32), in_=B_words[2 * j : 2 * j + 2].rearrange("g p n -> p g n").bitcast(I32))
            made["b_words", j] = words

        def load_c(j):
            for quad in range(4):
                nc.sync.dma_start(
                    out=made["scales", j][32 * quad : 32 * quad + 4, 2 * F :].bitcast(I32),
                    in_=C_scales[j, 4 * quad : 4 * quad + 4, :].bitcast(I32),
                )
            words = keep.tile([P, 2 * N], U8, name="c_words%d" % j, align_bytes=64)
            nc.sync.dma_start(out=words[:].bitcast(I32), in_=C_words[j].bitcast(I32))
            made["c_words", j] = words

        def load_rows(what, source, i, bufs):
            made[what, i] = work.tile([P, source.shape[1]], BF16, name=what, bufs=bufs)
            nc.sync.dma_start(out=made[what, i][:], in_=source[rows(i), :])

        def load_bar(i):
            load_rows("bar", bar_rows, i, 8)

        def load_image(i):
            load_rows("image", image_rows, i, 7)

        def load_dual(i):
            load_rows("dual", dual_rows, i, 4)

        def turn(pairs, passes, tag):
            turned = bank(tag, [P, 2 * len(passes), P])
            for s, g in enumerate(passes):
                for u in range(2):
                    nc.tensor.transpose(turned[:, 2 * s + u, :], pairs[:, PAIRS * g + u : PAIRS * (g + 1) : 2], ident[:])
            return turned

        def interleave(copy, name, turned, bufs):
            ordered = work.tile([P, turned.shape[1] // 2, HALF], BF16, name=name, bufs=bufs, align_bytes=64)
            copy(
                out=ordered[:].bitcast(F32).rearrange("p g (r u) -> p g r u", u=2),
                in_=turned[:].rearrange("p (g u) r -> p g r u", u=2),
            )
            return ordered

        def quantize(name, ordered, bufs):
            width = ordered.shape[1] * P
            codes = work.tile([P, width], U32, name=name + "_codes", bufs=bufs, align_bytes=64)
            scales = work.tile([P, width], U8, name=name + "_scales", bufs=bufs, align_bytes=64)
            nc.vector.quantize_mx(out=codes[:].bitcast(FP8X4), scales=scales[:], in_=ordered[:].rearrange("p g c -> p (g c)"))
            return codes, scales

        def turn_bar(i, tag="bar_t"):
            made["bar_t", i] = turn(made["bar", i][:].bitcast(F32), [0, 1], tag)

        def copy_bar(i, copy=on_scalar):
            made["bar_k", i] = interleave(copy, "bar_k", made["bar_t", i], 4)

        def quantize_bar(i):
            made["bar_q", i] = quantize("bar", made["bar_k", i], 3)

        def first_product(i, tag="r_acc"):
            j = i // PER_GROUP
            codes, scales = made["bar_q", i]
            acc = bank(tag, [P, F])
            for g in range(2):
                nc.tensor.matmul_mx(
                    out=acc[:],
                    lhsT=codes[:, rows(g)].bitcast(FP8X4),
                    lhsT_scale=scales[:, rows(g)],
                    rhs=made["b_words", j][:, g, :].bitcast(FP4X4),
                    rhs_scale=made["scales", j][:, F * g : F * (g + 1)],
                    start=(g == 0),
                    stop=(g == 1),
                )
            made["r_acc", i] = acc

        def residual(i):
            r = work.tile([P, F], BF16, name="r", bufs=4)
            nc.vector.tensor_tensor(
                out=r[:].rearrange("m (u p e) -> m u p e", u=2, e=2),
                in0=made["r_acc", i][:].rearrange("m (p u e) -> m u p e", u=2, e=2),
                in1=made["image", i][:].rearrange("m (p u e) -> m u p e", u=2, e=2),
                op=ALU.subtract,
            )
            made["r", i] = r

        def turn_r(i, tag="r_t"):
            turned = bank(tag, [P, 2, P])
            pairs = made["r", i][:].bitcast(F32)
            for u in range(2):
                nc.tensor.transpose(turned[:, u, :], pairs[:, rows(u)], ident[:])
            made["r_t", i] = turned

        def copy_r(i, copy):
            made["r_k", i] = interleave(copy, "r_k", made["r_t", i], 2)

        def quantize_r(i):
            made["r_q", i] = quantize("r", made["r_k", i], 4)

        def second_product(i, b):
            j = i // PER_GROUP
            codes, scales = made["r_q", i]
            acc = bank("h", [P, HALF])
            nc.tensor.matmul_mx(
                out=acc[:],
                lhsT=codes[:].bitcast(FP8X4),
                lhsT_scale=scales[:],
                rhs=made["c_words", j][:, 2 * HALF * b : 2 * HALF * (b + 1)].bitcast(FP4X4),
                rhs_scale=made["scales", j][:, 2 * F + HALF * b : 2 * F + HALF * (b + 1)],
                start=True,
                stop=True,
            )
            made["h", i, b] = acc

        def magnitude(i, b):
            if b == 0:
                made["mag", i] = work.tile([P, N], F32, name="mag")
            nc.scalar.activation(out=made["mag", i][:, half(b)], in_=made["h", i, b][:], func=ACT.Abs)

        def numerator(i, b):
            if b == 0:
                made["num", i] = work.tile([P, N], F32, name="num", bufs=3)
            nc.vector.tensor_tensor(
                out=made["num", i][:, half(b)], in0=made["dual", i][:, half(b)], in1=made["h", i, b][:], op=ALU.subtract
            )

        def inverse_root(i, lo, hi):
            if lo == 0:
                made["root", i] = work.tile([P, N], F32, name="root")
            nc.scalar.activation(
                out=made["root", i][:, lo:hi], in_=made["mag", i][:, lo:hi], func=ACT.Abs_reciprocal_sqrt, bias=1.0
            )

        def inverse(i, lo, hi):
            if lo == 0:
                made["inv", i] = work.tile([P, N], F32, name="inv", bufs=3)
            nc.scalar.activation(out=made["inv", i][:, lo:hi], in_=made["root", i][:, lo:hi], func=ACT.Square)

        def new_dual(engine, into, i, lo, hi):
            engine.tensor_tensor(
                out=into[:, N * i + lo : N * i + hi], in0=made["num", i][:, lo:hi], in1=made["inv", i][:, lo:hi], op=ALU.mult
            )

        def store_y(i, lo, hi):
            nc.sync.dma_start(out=y_rows[rows(i), lo:hi], in_=y_all[:, N * i + lo : N * i + hi])

        def round_y(lo, hi):
            nc.gpsimd.tensor_scalar(
                out=y_bf16[:, lo:hi], in0=y_all[:, lo:hi], scalar1=1.0, scalar2=1.0, op0=ALU.mult, op1=ALU.mult
            )

        def turn_y(halves, tag):
            made["y_t", halves[0]] = turn(y_bf16[:].bitcast(F32), halves, tag)

        def copy_y(halves, copy):
            ordered = interleave(copy, "y_k", made["y_t", halves[0]], 4)
            for s, h in enumerate(halves):
                made["y_k", h] = ordered[:, s, :]

        def store_words(first, last):
            j = first // PER_GROUP
            lo, hi = P * first, P * (last + 1)
            nc.sync.dma_start(
                out=out_1[:, :, lo:hi, :].rearrange("g p m t -> p g (m t)").bitcast(I32),
                in_=made["y_codes", j][:, :, lo - R * j : hi - R * j].bitcast(I32),
            )

        def store_scales(plane, first, last, queues):
            for quad in range(4):
                queues[quad].dma_start(
                    out=out_2[:, 4 * quad : 4 * quad + 4, P * first : P * (last + 1)].rearrange("g r m -> r g m").bitcast(I32),
                    in_=plane[32 * quad : 32 * quad + 4, :, :].bitcast(I32),
                )

        def quantize_y(h):
            i, g = divmod(h, 2)
            j, k = divmod(i, PER_GROUP)
            if k == 0 and g == 0:
                made["y_codes", j] = work.tile([P, 2, R], U32, name="y_codes", align_bytes=64)
            plane = y_scales_last[:, g, rows(k)] if j == G - 1 else y_scales_early[:, g, rows(i)]
            nc.vector.quantize_mx(out=made["y_codes", j][:, g, rows(k)].bitcast(FP8X4), scales=plane, in_=made["y_k", h])
            if g == 1 and k == PER_GROUP - 1 and j < G - 1:
                store_words(PER_GROUP * j, i)
            if g == 1 and i == LAST - PER_GROUP:
                store_scales(y_scales_early, 0, i, [nc.sync] * 4)
            if g == 1 and i == LAST - 2:
                store_words(PER_GROUP * j, i)

        def on(step, i, *rest):
            if 0 <= i < TILES:
                step(i, *rest)

        clear_scales(0)
        warm_in = keep.tile([P, 8], F32, name="warm_in")
        warm_out = keep.tile([P, 8], F32, name="warm_out")
        nc.vector.memset(warm_in[:], 1.0)
        nc.scalar.activation(out=warm_out[:], in_=warm_in[:], func=ACT.Abs_reciprocal_sqrt)
        make_identity(nc, ident[:])
        for j in range(1, G):
            clear_scales(j)

        load_bar(0)
        load_b(0)
        load_bar(1)
        load_image(0)
        load_bar(2)
        load_image(1)
        load_c(0)
        load_bar(3)
        load_dual(0)
        load_image(2)
        load_bar(4)
        load_dual(1)
        load_image(3)
        load_b(1)
        load_bar(5)
        load_image(4)
        load_bar(6)

        turn_bar(0, "r_acc")
        copy_bar(0, on_vector)
        quantize_bar(0)
        turn_bar(1, "h")
        first_product(0, "bar_t")
        copy_bar(1, on_vector)
        quantize_bar(1)
        first_product(1, "r_t")
        residual(0)
        turn_r(0, "bar_t")
        residual(1)
        copy_r(0, on_scalar)
        turn_bar(2, "r_acc")
        quantize_r(0)
        copy_bar(2, on_vector)
        turn_bar(3, "h")
        turn_r(1, "y_t")
        copy_bar(3, on_vector)
        second_product(0, 0)
        second_product(0, 1)
        quantize_bar(2)
        turn_bar(4, "r_t")
        magnitude(0, 0)
        copy_r(1, on_vector)
        quantize_r(1)
        first_product(2, "y_t")
        residual(2)

        rounded = 0
        turned = 0
        for n in range(TILES):
            ready = list(range(turned, rounded // HALF))
            turned += len(ready)
            two, third = ready[:2], ready[2:]
            split = VECTOR_COLUMNS if n - 1 < VECTOR_ALONE_FROM else N
            r_copy_on_scalar = n + 2 >= SCALAR_COPIES_R_FROM

            on(load_bar, n + 7)
            on(load_image, n + 5)
            on(load_dual, n + 2)
            if (n + 5) % PER_GROUP == 0 and n + 5 < TILES:
                load_b((n + 5) // PER_GROUP)
            if (n + 3) % PER_GROUP == 0 and n + 3 < TILES:
                load_c((n + 3) // PER_GROUP)

            if two:
                turn_y(two, "y_t")
            if third:
                turn_y(third, "bar_t")
            magnitude(n, 1)
            if n == LAST:
                copy_y(two, on_scalar)
            if n > 0:
                new_dual(nc.vector, y_all, n - 1, 0, split)
            on(quantize_bar, n + 3)
            on(second_product, n + 1, 0)
            if n + 4 < TILES:
                copy_bar(n + 4)
                inverse_root(n, 0, N)
            else:
                inverse_root(n, 0, HALF)
                inverse_root(n, HALF, N)
            on(turn_r, n + 2)
            on(second_product, n + 1, 1)
            if third:
                copy_y(third, on_vector)
            if r_copy_on_scalar:
                on(copy_r, n + 2, on_scalar)
            on(first_product, n + 3)
            numerator(n, 0)
            if not r_copy_on_scalar:
                copy_r(n + 2, on_vector)
            if two and n < LAST:
                copy_y(two, on_vector)
            on(magnitude, n + 1, 0)
            on(turn_bar, n + 5)
            numerator(n, 1)
            on(residual, n + 3)
            on(quantize_r, n + 2)
            if n > 0:
                round_y(rounded, N * (n - 1) + split)
                rounded = N * (n - 1) + split
                if split < N:
                    new_dual(nc.gpsimd, y_all, n - 1, split, N)
                store_y(n - 1, 0, N)
            if n < LAST:
                inverse(n, 0, N)
            else:
                inverse(n, 0, HALF)
                inverse(n, HALF, N)
            for h in ready:
                quantize_y(h)

        before_last = list(range(turned, 2 * LAST))
        turn_y(before_last, "y_t")
        copy_y(before_last, on_scalar)
        for b, tag in enumerate(["r_t", "bar_t"]):
            new_dual(nc.vector, y_bf16, LAST, HALF * b, HALF * (b + 1))
            turn_y([2 * LAST + b], tag)
            copy_y([2 * LAST + b], on_scalar)
        for b in range(2):
            new_dual(nc.vector, y_all, LAST, HALF * b, HALF * (b + 1))
            store_y(LAST, HALF * b, HALF * (b + 1))
        for h in range(turned, 2 * TILES):
            quantize_y(h)
        store_words(LAST - 1, LAST)
        store_scales(y_scales_last, TILES - PER_GROUP, LAST, [nc.scalar, nc.scalar, nc.sync, nc.sync])
